import numpy as np
import ml_dtypes


def mxq(x, axis, fmt="e4m3"):
    dtype, down = {"e4m3": (ml_dtypes.float8_e4m3fn, 7), "e5m2": (ml_dtypes.float8_e5m2, 14)}[fmt]
    v = np.moveaxis(np.asarray(x, np.float32).astype(ml_dtypes.bfloat16).astype(np.float64), axis, -1)
    blocks = v.reshape(v.shape[:-1] + (-1, 32))
    amax = np.abs(blocks).max(-1, keepdims=True)
    byte = np.maximum(np.where(amax > 0, np.frexp(amax)[1] - 1 + 127, 0) - down, 1)
    scale = np.exp2(byte - 127.0)
    codes = (blocks / scale).astype(np.float32).astype(dtype).astype(np.float64)
    return np.moveaxis((codes * scale).reshape(v.shape), -1, axis)


WIDE = False


def mx_kscale(k):
    if not WIDE:
        return np.ones(k)
    levels = np.array([30, -30])
    if k % 512:
        return np.exp2(np.random.permutation(np.resize(levels, k // 32))).repeat(32)
    a = np.empty((k // 512, 16))
    for p in range(k // 512):
        a[p, :8] = np.random.permutation(np.resize(levels, 8))
        for g in range(8):
            far = levels[np.abs(levels - a[p, g]) >= 10]
            a[p, g + 8] = far[np.random.randint(len(far))]
    return np.exp2(a.ravel()).repeat(32)


BF16 = ml_dtypes.bfloat16


def bf(x):
    return np.asarray(x, np.float32).astype(BF16)


def f64(x):
    return np.asarray(x).astype(np.float64)


C, N, R, P = 512, 2048, 512, 1024


def setup_inputs():
    s, t = mx_kscale(C), mx_kscale(N)
    return {"u": bf(np.random.standard_normal((C, P)) / s[:, None]),
            "r": bf(np.random.standard_normal((N, P))),
            "w1": bf(np.random.standard_normal((N, C)) / np.sqrt(C) * s),
            "g1": bf(1 + 0.1 * np.random.standard_normal(N)),
            "b1": bf(0.3 * np.random.standard_normal(N)),
            "d": bf((1 + 0.1 * np.random.standard_normal(N)) * t),
            "w2": bf(np.random.standard_normal((R, N)) / np.sqrt(N) / t),
            "g2": bf(1 + 0.1 * np.random.standard_normal(R)),
            "b2": bf(0.3 * np.random.standard_normal(R))}


def relu(v):
    return np.maximum(v, 0.0)


def reference(u, r, w1, g1, b1, d, w2, g2, b2):
    a = mxq(f64(w1), 1, "e4m3") @ mxq(f64(u), 0, "e4m3")
    y = relu(a * f64(g1)[:, None] + f64(b1)[:, None] + f64(r))
    h = y * f64(d)[:, None]
    c = mxq(f64(w2), 1, "e4m3") @ mxq(h, 0, "e5m2")
    z = relu(c * f64(g2)[:, None] + f64(b2)[:, None])
    return y, z

from contextlib import ExitStack

import concourse.mybir as mybir
from concourse.masks import make_identity

C, N, R, PIX = 512, 2048, 512, 1024
FLOPS = 2 * N * C * PIX + 2 * R * N * PIX
BYTES = 2 * (C * PIX + N * PIX + N * C + R * N + 3 * N + 2 * R) + 4 * (N * PIX + R * PIX)

F32 = mybir.dt.float32
BF16 = mybir.dt.bfloat16
U32 = mybir.dt.uint32
U8 = mybir.dt.uint8
E4M3 = mybir.dt.float8_e4m3fn_x4
E5M2 = mybir.dt.float8_e5m2_x4
ACT = mybir.ActivationFunctionType
ALU = mybir.AluOpType

P = 128
HALF = 512
GROUPS = N // 512
UNITS = 2 * GROUPS
SLOTS = 4 * UNITS
HD = ["sggs","ssgg","sgsg","ggsg","sggs","gsgs","sssg","cccc"]
WENG = {1:"ss",2:"ss",3:"ss",4:"ss",5:"ss",6:"ss",7:"ss"}
ZE = ["ssss", "svss"]
ORDER = [(0, 0), (0, 1), (1, 0), (1, 1), (2, 0), (3, 0), (2, 1), (3, 1)]
U1 = [1,1]
IQ = [[5,7],[10,11],[13,15],[17,19],[21,22],[26,27],[29,30]]
Z0 = 29
LAST = [0,512]
PF = 2
USPLIT = 320
PREP = {1:[1,1,3],2:[4,4,7],3:[8,10,13],4:[7,11,14],5:[12,13,25],6:[12,15,24],7:[14,20,25]}
MM2 = {0:26,1:30,2:26,3:31,4:27,5:29,6:31}


def tile_bottleneck_junction_convs_f3_kernel(tc, u, r, w1, g1, b1, d, w2, g2, b2, out_y, out_z):
    nc = tc.nc
    with ExitStack() as ctx:
        keep = ctx.enter_context(tc.tile_pool(name="keep", bufs=1))
        stage = ctx.enter_context(tc.tile_pool(name="stage", bufs=2))
        ypool = ctx.enter_context(tc.tile_pool(name="ypool", bufs=4))
        psum = ctx.enter_context(tc.psum_pool(name="psum", bufs=1))
        ctx.enter_context(tc.manual_schedule())

        ident = keep.tile([P, P], F32, name="ident")
        vecs = keep.tile([P, 512], BF16, name="vecs")
        warm = keep.tile([P, 1], F32, name="warm")
        vwords = keep.tile([P, 2, 16], F32, name="vwords")
        vec = keep.tile([P, 16, 4], F32, name="vec")
        w1_raw = [keep.tile([P, 2048], BF16, name="w1_raw%d" % g) for g in range(4)]
        w2_raw = [keep.tile([P, 2048], BF16, name="w2_raw%d" % g) for g in range(4)]
        raw = w1_raw + w2_raw
        u_raw = [keep.tile([P, 4, HALF], BF16, name="u_raw%d" % h) for h in range(2)]
        r_half = [keep.tile([P, 4, HALF], BF16, name="r_half%d" % h) for h in range(2)]
        r_full = [None] + [keep.tile([P, 4, PIX], BF16, name="r_full%d" % g) for g in range(1, 4)]
        w_codes = [keep.tile([P, 512], U32, name="w_codes%d" % c, align_bytes=64) for c in range(8)]
        w_scales = [keep.tile([P, 512], U8, name="w_scales%d" % c, align_bytes=64) for c in range(8)]
        u_codes = [keep.tile([P, HALF], U32, name="u_codes%d" % h, align_bytes=64) for h in range(2)]
        u_scales = [keep.tile([P, HALF], U8, name="u_scales%d" % h, align_bytes=64) for h in range(2)]
        h_codes = [keep.tile([P, HALF], U32, name="h_codes%d" % k, align_bytes=64) for k in range(UNITS)]
        h_scales = [keep.tile([P, HALF], U8, name="h_scales%d" % k, align_bytes=64) for k in range(UNITS)]

        nc.vector.memset(vecs[:].bitcast(F32), 0.0)
        nc.vector.memset(warm[:], 0.0)
        for row, v, n in ((0, g1, 4), (4, b1, 4), (8, d, 4), (12, g2, 1), (13, b2, 1)):
            nc.scalar.dma_start(out=vecs[row : row + n, :], in_=v.rearrange("(g x) -> g x", g=n))
        make_identity(nc, ident[:])
        nc.scalar.activation(warm[:], warm[:], ACT.Relu)

        def load_w1(g):
            nc.sync.dma_start(
                out=w1_raw[g][:], in_=w1[512 * g : 512 * (g + 1), :].rearrange("(m t) k -> m (t k)", t=4)
            )

        def load_w1_part(b):
            nc.sync.dma_start(
                out=w1_raw[0][:, 1024 * b : 1024 * (b + 1)],
                in_=w1[0:512, :].rearrange("(m t) k -> m (t k)", t=4)[:, 1024 * b : 1024 * (b + 1)],
            )

        u_view = u.rearrange("(p j) w -> p j w", j=4)
        r_view = r.rearrange("(g p t) w -> g p t w", g=GROUPS, t=4)
        y_view = out_y.rearrange("(g p t) w -> g p t w", g=GROUPS, t=4)
        z_view = out_z.rearrange("(p i) w -> p i w", i=4)
        w2_view = w2.rearrange("(m i) k -> i m k", i=4)

        load_w1_part(0)
        nc.sync.dma_start(out=u_raw[0][:], in_=u_view[:, :, 0:HALF])
        load_w1_part(1)
        nc.sync.dma_start(out=r_half[0][:], in_=r_view[0][:, :, 0:HALF])
        nc.sync.dma_start(out=u_raw[1][:], in_=u_view[:, :, HALF:PIX])
        load_w1(1)
        nc.sync.dma_start(out=r_half[1][:], in_=r_view[0][:, :, HALF:PIX])
        nc.sync.dma_start(out=r_full[1][:], in_=r_view[1])
        load_w1(2)
        nc.sync.dma_start(out=w2_raw[0][:], in_=w2_view[0])
        load_w1(3)
        nc.sync.dma_start(out=w2_raw[1][:], in_=w2_view[1])
        nc.sync.dma_start(out=r_full[2][:], in_=r_view[2])
        nc.sync.dma_start(out=w2_raw[2][:], in_=w2_view[2])
        nc.sync.dma_start(out=w2_raw[3][:], in_=w2_view[3])
        nc.sync.dma_start(out=r_full[3][:], in_=r_view[3])

        grouped = {}

        def w_transpose(c, banks=(0, 1)):
            words = raw[c][:].bitcast(F32)
            tiles = grouped.setdefault(c, [])
            for b in banks:
                pt = psum.tile([P, 2, 2, P], F32, name="pt%d_%d" % (c, b), tag="acc%d" % (2 * (c % 2) + b))
                for s in range(2):
                    for e in range(2):
                        base = 256 * (2 * b + s) + e
                        nc.tensor.transpose(pt[:, s, e, :], words[:, base : 256 * (2 * b + s + 1) : 2], ident[:])
                tiles.append(pt)

        wg = {}

        def w_copy(c, engines, banks=(0, 1)):
            if c not in wg:
                wg[c] = stage.tile([P, 2048], BF16, name="wg%d" % c, tag="wg", align_bytes=64, bufs=3)
            g32 = wg[c][:].bitcast(F32).rearrange("p (b s m e) -> p b s m e", b=2, s=2, e=2)
            for b in banks:
                src = grouped[c][b][:].rearrange("p s e m -> p s m e")
                if engines[b] == "v":
                    nc.vector.tensor_copy(out=g32[:, b], in_=src)
                else:
                    nc.scalar.copy(out=g32[:, b], in_=src)

        def w_quant(c, lo=0, hi=512):
            nc.vector.quantize_mx(
                out=w_codes[c][:, lo:hi].bitcast(E4M3), scales=w_scales[c][:, lo:hi], in_=wg[c][:, 4 * lo : 4 * hi]
            )

        u_grouped = [stage.tile([P, HALF, 4], BF16, name="ug%d" % h, tag="ug", align_bytes=64) for h in range(2)]

        def u_interleave(h, lo, hi, eng):
            dst = u_grouped[h][:, lo:hi, :].rearrange("p (c i) j -> p c j i", i=4)
            src = u_raw[h][:, :, lo:hi].rearrange("p j (c i) -> p c j i", i=4)
            if eng == "v":
                nc.vector.tensor_copy(out=dst, in_=src)
            else:
                nc.scalar.copy(out=dst, in_=src)

        def u_quant(h):
            nc.vector.quantize_mx(
                out=u_codes[h][:].bitcast(E4M3),
                scales=u_scales[h][:],
                in_=u_grouped[h][:].rearrange("p w j -> p (w j)"),
            )

        a_tiles = {}

        def mm1(s):
            k, t = divmod(s, 4)
            g, h = ORDER[k]
            a = psum.tile([P, HALF], F32, name="a%d" % s, tag="a%d" % t)
            nc.tensor.matmul_mx(
                out=a[:],
                lhsT=w_codes[g][:, P * t : P * (t + 1)].bitcast(E4M3),
                lhsT_scale=w_scales[g][:, P * t : P * (t + 1)],
                rhs=u_codes[h][:].bitcast(E4M3),
                rhs_scale=u_scales[h][:],
                start=True,
                stop=True,
            )
            a_tiles[s] = a

        t32, yt, hd, hb = {}, {}, {}, {}

        def add_residual(s, lo=0, hi=HALF):
            k, t = divmod(s, 4)
            g, h = ORDER[k]
            if t == 0 and lo == 0:
                t32[k] = stage.tile([P, 4, HALF], F32, name="t32_%d" % k, tag="t32")
            res = r_half[h][:, t, lo:hi] if g == 0 else r_full[g][:, t, HALF * h + lo : HALF * h + hi]
            nc.vector.scalar_tensor_tensor(
                out=t32[k][:, t, lo:hi], in0=a_tiles[s][:, lo:hi], scalar=vec[:, g, t : t + 1], in1=res, op0=ALU.mult, op1=ALU.add
            )

        def relu_y(s, lo=0, hi=HALF):
            k, t = divmod(s, 4)
            g = ORDER[k][0]
            if t == 0 and lo == 0:
                yt[k] = ypool.tile([P, 4, HALF], F32, name="y%d" % k, tag="y")
                hd[k] = stage.tile([P, 4, HALF], BF16, name="hd%d" % k, tag="hd")
            nc.scalar.activation(yt[k][:, t, lo:hi], t32[k][:, t, lo:hi], ACT.Relu, bias=vec[:, 4 + g, t : t + 1])

        def scale_d(s, lo=0, hi=HALF):
            k, t = divmod(s, 4)
            g = ORDER[k][0]
            e = HD[k][t]
            dst, src, col = hd[k][:, t, lo:hi], yt[k][:, t, lo:hi], vec[:, 8 + g, t : t + 1]
            if e == "s":
                nc.scalar.activation(dst, src, ACT.Copy, scale=col)
            elif e == "g":
                nc.gpsimd.tensor_scalar(out=dst, in0=src, scalar1=col, scalar2=0.0, op0=ALU.mult, op1=ALU.add)
            elif e == "v":
                nc.vector.tensor_scalar(out=dst, in0=src, scalar1=col, scalar2=None, op0=ALU.mult)

        def store_y(k):
            g, h = ORDER[k]
            nc.sync.dma_start(out=y_view[g][:, :, HALF * h : HALF * (h + 1)], in_=yt[k][:])

        def h_interleave(k, lo=0, hi=HALF):
            if lo == 0:
                hb[k] = stage.tile([P, HALF, 4], BF16, name="hb%d" % k, tag="hb", align_bytes=64)
            if HD[k] == "cccc":
                nc.vector.tensor_tensor(
                    out=hb[k][:, lo:hi, :],
                    in0=yt[k][:, :, lo:hi].rearrange("p t n -> p n t"),
                    in1=vec[:, 8 + ORDER[k][0], :].unsqueeze(1).to_broadcast([P, hi - lo, 4]),
                    op=ALU.mult,
                )
            else:
                nc.vector.tensor_copy(
                    out=hb[k][:, lo:hi, :].rearrange("p (c i) t -> p c t i", i=4),
                    in_=hd[k][:, :, lo:hi].rearrange("p t (c i) -> p c t i", i=4),
                )

        def h_quant(k, lo=0, hi=HALF):
            nc.vector.quantize_mx(
                out=h_codes[k][:, lo:hi].bitcast(E5M2),
                scales=h_scales[k][:, lo:hi],
                in_=hb[k][:, lo:hi, :].rearrange("p n t -> p (n t)"),
            )

        acc = {}

        def mm2(k):
            g, h = ORDER[k]
            for i in range(4):
                if g == 0:
                    acc[i] = psum.tile([P, HALF], F32, name="acc_%d_%d" % (h, i), tag="acc%d" % i)
                nc.tensor.matmul_mx(
                    out=acc[i][:],
                    lhsT=w_codes[4 + i][:, P * g : P * (g + 1)].bitcast(E4M3),
                    lhsT_scale=w_scales[4 + i][:, P * g : P * (g + 1)],
                    rhs=h_codes[k][:].bitcast(E5M2),
                    rhs_scale=h_scales[k][:],
                    start=(g == 0),
                    stop=(g == GROUPS - 1),
                )

        def finish_z(h):
            zt = stage.tile([P, 4, HALF], F32, name="z%d" % h, tag="z")
            for i in range(4):
                if ZE[h][i] == "s":
                    nc.scalar.activation(
                        zt[:, i, :], acc[i][:], ACT.Relu, bias=vec[:, 13, i : i + 1], scale=vec[:, 12, i : i + 1]
                    )
                else:
                    nc.vector.tensor_scalar(
                        out=zt[:, i, :], in0=acc[i][:], scalar1=vec[:, 12, i : i + 1], scalar2=vec[:, 13, i : i + 1], op0=ALU.mult, op1=ALU.add
                    )
                    nc.vector.tensor_scalar(out=zt[:, i, :], in0=zt[:, i, :], scalar1=0.0, scalar2=None, op0=ALU.max)
                if h == 1:
                    nc.sync.dma_start(out=z_view[:, i, HALF * h : HALF * (h + 1)], in_=zt[:, i, :])
            if h == 0:
                nc.sync.dma_start(out=z_view[:, :, HALF * h : HALF * (h + 1)], in_=zt[:])

        w_transpose(0, (0,))
        pv = psum.tile([P, 2, P], F32, name="pv", tag="a3")
        vwords_in = vecs[:].bitcast(F32)
        for e in range(2):
            nc.tensor.transpose(pv[:, e, :], vwords_in[:, e:256:2], ident[:])
        w_transpose(0, (1,))
        w_copy(0, "ss", (0,))
        u_interleave(0, 0, USPLIT, "v")
        u_interleave(0, USPLIT, HALF, "s")
        nc.scalar.copy(out=vwords[:], in_=pv[:, :, 0:16])
        w_copy(0, "ss", (1,))
        w_quant(0, 0, 256)
        u_quant(0)
        w_quant(0, 256, 512)
        nc.vector.tensor_copy(
            out=vec[:].rearrange("p r (e f) -> p e r f", e=2),
            in_=vwords[:].bitcast(BF16).rearrange("p e (r f) -> p e r f", f=2),
        )
        for s in range(PF):
            mm1(s)

        todo = {}
        for c in range(1, 8):
            st, sc, sq = PREP[c]
            todo.setdefault(st, []).append((w_transpose, (c,)))
            todo.setdefault(sc, []).append((w_copy, (c, WENG.get(c, "ss"))))
            todo.setdefault(sq, []).append((w_quant, (c,)))
        todo.setdefault(U1[0], []).append((u_interleave, (1, 0, HALF, "v")))
        todo.setdefault(U1[1], []).append((u_quant, (1,)))
        for k in range(7):
            todo.setdefault(IQ[k][0], []).append((h_interleave, (k,)))
            todo.setdefault(IQ[k][1], []).append((h_quant, (k,)))
        for k, s in MM2.items():
            todo.setdefault(s, []).append((mm2, (k,)))
        todo.setdefault(Z0, []).append((finish_z, (0,)))

        for s in range(28):
            mm1(s + PF)
            add_residual(s)
            relu_y(s)
            if s % 4:
                scale_d(s - 1)
            if s % 4 == 3:
                scale_d(s)
                store_y(s // 4)
            for f, args in todo.get(s, []):
                f(*args)
        cuts = LAST
        for s in range(28 + PF, SLOTS):
            mm1(s)
        for n in range(len(cuts) - 1):
            lo, hi = cuts[n], cuts[n + 1]
            for s in range(28, 32):
                add_residual(s, lo, hi)
                relu_y(s, lo, hi)
                if s > 28:
                    scale_d(s - 1, lo, hi)
                if n == 0:
                    for f, args in todo.get(s, []):
                        f(*args)
            scale_d(31, lo, hi)
            if n > 0:
                h_interleave(7, cuts[n - 1], lo)
                h_quant(7, cuts[n - 1], lo)
        store_y(7)
        h_interleave(7, cuts[-2], HALF)
        h_quant(7, cuts[-2], HALF)
        mm2(7)
        finish_z(1)
